import numpy as np
import ml_dtypes


def mxq(x, axis, fmt="e4m3"):
    dtype, down = {"e4m3": (ml_dtypes.float8_e4m3fn, 7), "e5m2": (ml_dtypes.float8_e5m2, 14)}[fmt]
    v = np.moveaxis(np.asarray(x, np.float32).astype(ml_dtypes.bfloat16).astype(np.float64), axis, -1)
    blocks = v.reshape(v.shape[:-1] + (-1, 32))
    amax = np.abs(blocks).max(-1, keepdims=True)
    byte = np.maximum(np.where(amax > 0, np.frexp(amax)[1] - 1 + 127, 0) - down, 1)
    scale = np.exp2(byte - 127.0)
    codes = (blocks / scale).astype(np.float32).astype(dtype).astype(np.float64)
    return np.moveaxis((codes * scale).reshape(v.shape), -1, axis)


WIDE = False


def mx_kscale(k):
    if not WIDE:
        return np.ones(k)
    levels = np.array([30, -30])
    if k % 512:
        return np.exp2(np.random.permutation(np.resize(levels, k // 32))).repeat(32)
    a = np.empty((k // 512, 16))
    for p in range(k // 512):
        a[p, :8] = np.random.permutation(np.resize(levels, 8))
        for g in range(8):
            far = levels[np.abs(levels - a[p, g]) >= 10]
            a[p, g + 8] = far[np.random.randint(len(far))]
    return np.exp2(a.ravel()).repeat(32)


def f64(x):
    return np.asarray(x).astype(np.float64)


def striped(idx):
    return np.tile(np.asarray(idx).reshape(-1, 16).T, (8, 1)).astype(np.uint16)


def unstriped(offs):
    return offs[:16].T.reshape(-1).astype(np.int64)


E2M1 = np.array([0.0, 0.5, 1.0, 1.5, 2.0, 3.0, 4.0, 6.0, -0.0, -0.5, -1.0, -1.5, -2.0, -3.0, -4.0, -6.0])


def pack_weight(w, fmt):
    k, n = w.shape
    w = f64(np.asarray(w, np.float32).astype(ml_dtypes.bfloat16)).reshape(k // 32, 32, n)
    amax = np.abs(w).max(1)
    if fmt == "e4m3":
        byte = np.frexp(amax)[1] - 1 + 127 - 7
    else:
        mant, ex = np.frexp(amax / 6.0)
        byte = np.where(mant > 0.5, ex, ex - 1) + 127
    byte = np.clip(np.where(amax > 0, byte, 1), 1, 254)
    scaled = (w * np.exp2(127.0 - byte)[:, None, :]).reshape(k, n).astype(np.float32)
    by_word = np.ascontiguousarray(scaled.reshape(k // 512, 128, 4, n).transpose(0, 1, 3, 2))
    if fmt == "e4m3":
        words = by_word.astype(ml_dtypes.float8_e4m3fn).view(np.uint8)
    else:
        c = by_word.astype(ml_dtypes.float4_e2m1fn).view(np.uint8) & 0xF
        words = (c[..., 0::2] | (c[..., 1::2] << 4)).reshape(k // 512, 128, 2 * n)
    return np.ascontiguousarray(words), np.ascontiguousarray(byte.astype(np.uint8).reshape(k // 512, 16, n))


def unpack_weight(words, scales, fmt):
    g, _, n = scales.shape
    words = np.ascontiguousarray(words).reshape(g, 128, n, -1)
    if fmt == "e4m3":
        vals = words.view(ml_dtypes.float8_e4m3fn).astype(np.float64)
    else:
        nib = np.empty((g, 128, n, 4), np.uint8)
        nib[..., 0::2] = words & 0xF
        nib[..., 1::2] = words >> 4
        vals = E2M1[nib]
    vals = vals * np.repeat(np.exp2(scales.astype(np.float64) - 127.0), 8, axis=1)[..., None]
    return vals.transpose(0, 1, 3, 2).reshape(g * 512, n)


K, T, J, R, C, O, N, E = 512, 2048, 256, 512, 512, 256, 256, 1024


def setup_inputs():
    n = np.random.standard_normal
    idx = np.random.permutation(T)[:J]
    idx2 = np.random.permutation(T)[:J]
    idx3 = np.random.permutation(C)[:J]
    idx4 = np.random.permutation(C)[:J]
    idx5 = np.random.permutation(C)[:O]
    idx6 = np.random.permutation(C)[:O]
    idx7 = np.random.permutation(E)[:O]
    fk = mx_kscale(K)
    fr = mx_kscale(R)
    xtp = pack_weight(n((K, T)) / fk[:, None], "e2m1")
    wp = pack_weight(n((K, R)) * 1 / np.sqrt(K) * fk[:, None] * fr, "e4m3")
    wbp = pack_weight(n((R, N)) * 1 / np.sqrt(R) / fr[:, None], "e2m1")
    return {
        "xt_words": xtp[0],
        "xt_scales": xtp[1],
        "w_words": wp[0],
        "w_scales": wp[1],
        "sa": (np.random.uniform(0.5, 1.6, (R, 1))).astype(np.float32),
        "wb_words": wbp[0],
        "wb_scales": wbp[1],
        "tz": (np.random.randint(-9, 10, (N, E)).astype(np.float64)).astype(np.float32),
        "so": (np.random.uniform(0.1, 0.3, (N, 1))).astype(np.float32),
        "offs": striped(idx),
        "offs2": striped(idx2),
        "offs3": striped(idx3),
        "offs4": striped(idx4),
        "offs5": striped(idx5),
        "offs6": striped(idx6),
        "offs7": striped(idx7),
    }


def reference(xt_words, xt_scales, w_words, w_scales, sa, wb_words, wb_scales, tz, so, offs, offs2, offs3, offs4, offs5, offs6, offs7):
    idx = unstriped(offs)
    idx2 = unstriped(offs2)
    idx3 = unstriped(offs3)
    idx4 = unstriped(offs4)
    idx5 = unstriped(offs5)
    idx6 = unstriped(offs6)
    idx7 = unstriped(offs7)
    xtu = unpack_weight(xt_words, xt_scales, "e2m1")
    wu = unpack_weight(w_words, w_scales, "e4m3")
    wbu = unpack_weight(wb_words, wb_scales, "e2m1")
    xtidxg = xtu[:, idx]
    a = wu.T @ xtidxg
    xtidx2g = xtu[:, idx2]
    b = wu.T @ xtidx2g
    pw = np.zeros((R, C))
    pw[:, idx3] = a
    pv = np.zeros((R, C))
    pv[:, idx4] = b
    pg = pw + pv
    hid = np.maximum(pg[:, idx5] * f64(sa), pg[:, idx6])
    hidq = mxq(hid, 0, "e5m2")
    p = wbu.T @ hidq
    y = np.maximum(p, f64(tz)[:, idx7] * f64(so))
    return y

@@ -1,0 +1,192 @@
+from contextlib import ExitStack
+
+import concourse.mybir as mybir
+
+K, T, J, R, C, O, N, E = 512, 2048, 256, 512, 512, 256, 256, 1024
+FLOPS = 2 * K * R * 2 * J + 2 * R * N * O
+
+F32 = mybir.dt.float32
+BF16 = mybir.dt.bfloat16
+I32 = mybir.dt.int32
+U32 = mybir.dt.uint32
+U16 = mybir.dt.uint16
+U8 = mybir.dt.uint8
+E4M3X4 = mybir.dt.float8_e4m3fn_x4
+E5M2X4 = mybir.dt.float8_e5m2_x4
+E2M1X4 = mybir.dt.float4_e2m1fn_x4
+COPY = mybir.ActivationFunctionType.Copy
+ADD = mybir.AluOpType.add
+MAX = mybir.AluOpType.max
+
+P = 128
+PACK = 4
+HALF = O // 2
+
+
+def load_scale_rows(queue, plane, scales):
+    for q in range(4):
+        queue.dma_start(
+            out=plane[32 * q : 32 * q + 4, :].bitcast(I32),
+            in_=scales[0, 4 * q : 4 * q + 4, :].bitcast(I32),
+        )
+
+
+def tile_list_sumboardweighed_tied_one_stepfloor_kernel(
+    tc, xt_words, xt_scales, w_words, w_scales, sa, wb_words, wb_scales, tz, so,
+    offs, offs2, offs3, offs4, offs5, offs6, offs7, out,
+):
+    nc = tc.nc
+    with ExitStack() as ctx:
+        keep = ctx.enter_context(tc.tile_pool(name="keep", bufs=1))
+        psum = ctx.enter_context(tc.psum_pool(name="psum", bufs=1))
+
+        def load_list(name, src):
+            tile = keep.tile([P, J // 16], U16, name=name)
+            nc.sync.dma_start(tile[:], src)
+            return tile
+
+        w_plane = keep.tile([P, R], U8, align_bytes=64, tag="w_plane")
+        xt_plane = keep.tile([P, T], U8, align_bytes=64, tag="xt_plane")
+        wb_plane = keep.tile([P, N], U8, align_bytes=64)
+        nc.vector.memset(xt_plane[:].bitcast(I32), 0)
+        nc.vector.memset(w_plane[:].bitcast(I32), 0)
+
+        xt_codes = keep.tile([P, T], U16, align_bytes=64, tag="xt_codes")
+        nc.scalar.dma_start(out=xt_codes[:].bitcast(I32), in_=xt_words[0].bitcast(I32))
+        load_scale_rows(nc.scalar, xt_plane, xt_scales)
+        list_a = load_list("list_a", offs)
+        w_stage = keep.tile([4, 4, R // 4], I32, align_bytes=64, tag="w_stage")
+        nc.sync.dma_start(out=w_stage[:], in_=w_scales[0].bitcast(I32).rearrange("(q r) c -> r q c", r=4))
+        list_b = load_list("list_b", offs2)
+        put_a = load_list("put_a", offs3)
+        put_b = load_list("put_b", offs4)
+        pick_scaled = load_list("pick_scaled", offs5)
+        w_codes = keep.tile([P, R], U32, align_bytes=64, tag="w_codes")
+        nc.sync.dma_start(
+            out=w_codes[:].bitcast(I32),
+            in_=w_words[0].rearrange("p c t -> p (c t)").bitcast(I32),
+        )
+        pick_plain = load_list("pick_plain", offs6)
+        pick_tz = load_list("pick_tz", offs7)
+
+        pw = [keep.tile([P, C], F32, name="pw%d" % s) for s in range(2)] * 2
+        pv = [keep.tile([P, C], F32, name="pv%d" % s) for s in range(2)] * 2
+        for s in range(2):
+            nc.vector.memset(pw[s][:], 0.0)
+            nc.vector.memset(pv[s][:], 0.0)
+        nc.vector.memset(wb_plane[:].bitcast(I32), 0)
+        for q in range(4):
+            nc.vector.tensor_copy(out=w_plane[32 * q : 32 * q + 4, :].bitcast(I32), in_=w_stage[:, q, :])
+
+        w_dealt = keep.tile([P, PACK, P], U32, align_bytes=64, tag="w_dealt")
+        nc.scalar.copy(
+            out=w_dealt[:].rearrange("p t m -> p m t"),
+            in_=w_codes[:].rearrange("p (m t) -> p m t", t=PACK),
+        )
+        w_plane_dealt = keep.tile([P, PACK, P], U8, align_bytes=64)
+        nc.vector.tensor_copy(
+            out=w_plane_dealt[:],
+            in_=w_plane[:].rearrange("p (m t) -> p t m", t=PACK),
+        )
+
+        banks = {}
+        for side, picks in (("a", list_a), ("b", list_b)):
+            codes = keep.tile([P, J], U16, align_bytes=64, name="codes_" + side)
+            plane = keep.tile([P, J], U8, align_bytes=64, name="plane_" + side)
+            nc.vector.tensor_copy(out=codes[:], in_=xt_codes[:].indirect(picks[:]))
+            nc.vector.tensor_copy(out=plane[:], in_=xt_plane[:].indirect(picks[:]))
+            for t in range(PACK):
+                bank = psum.tile([P, J], F32, name="bank_%s%d" % (side, t))
+                nc.tensor.matmul_mx(
+                    out=bank[:],
+                    lhsT=w_dealt[:, t, :].bitcast(E4M3X4),
+                    lhsT_scale=w_plane_dealt[:, t, :],
+                    rhs=codes[:].bitcast(E2M1X4),
+                    rhs_scale=plane[:],
+                    start=True,
+                    stop=True,
+                )
+                banks[(side, t)] = bank
+
+        sa_cols = keep.tile([P, PACK], F32, align_bytes=64, tag="w_plane")
+        nc.sync.dma_start(out=sa_cols[:], in_=sa.rearrange("(p t) o -> p (t o)", t=PACK))
+        wb_codes = keep.tile([P, 2 * N], U8, align_bytes=64, tag="xt_plane")
+        nc.sync.dma_start(out=wb_codes[:].bitcast(I32), in_=wb_words[0].bitcast(I32))
+        load_scale_rows(nc.sync, wb_plane, wb_scales)
+        so_cols = keep.tile([P, N // P], F32, align_bytes=64, tag="w_stage")
+        with nc.allow_non_contiguous_dma(reason="one step a partition"):
+            nc.sync.dma_start(out=so_cols[:], in_=so.rearrange("(b p) o -> p (b o)", p=P))
+        tz_rows = []
+        for b in range(N // P):
+            rows = keep.tile([P, E], F32, name="tz_rows%d" % b, align_bytes=64, tag=("w_codes", "xt_codes")[b])
+            nc.sync.dma_start(out=rows[:], in_=tz[b * P : (b + 1) * P, :])
+            tz_rows.append(rows)
+
+        a_rows = [keep.tile([P, J], F32, name="a_rows%d" % t) for t in range(PACK)]
+        b_rows = [keep.tile([P, J], F32, name="b_rows%d" % t) for t in range(PACK)]
+        pg = [keep.tile([P, C], F32, name="pg%d" % t, tag="pg%d" % t) for t in range(PACK)]
+        scaled = keep.tile([P, PACK, O], F32)
+        plain = keep.tile([P, PACK, O], F32)
+
+        def pick(t):
+            nc.scalar.activation(
+                out=scaled[:, t, :], in_=pg[t][:].indirect(pick_scaled[:]), func=COPY,
+                scale=sa_cols[:, t : t + 1],
+            )
+            if t in (0, PACK - 1):
+                nc.vector.tensor_copy(out=plain[:, t, :], in_=pg[t][:].indirect(pick_plain[:]))
+            else:
+                nc.scalar.activation(out=plain[:, t, :], in_=pg[t][:].indirect(pick_plain[:]), func=COPY)
+
+        nc.scalar.copy(out=a_rows[0][:], in_=banks[("a", 0)][:])
+        nc.vector.tensor_copy(out=a_rows[1][:], in_=banks[("a", 1)][:])
+        nc.vector.tensor_copy(out=b_rows[0][:], in_=banks[("b", 0)][:])
+        for t in range(PACK):
+            nc.scalar.activation(out=pw[t][:].indirect(put_a[:]), in_=a_rows[t][:], func=COPY)
+            nc.vector.tensor_copy(out=pv[t][:].indirect(put_b[:]), in_=b_rows[t][:])
+            if t + 1 < PACK:
+                nc.scalar.copy(out=b_rows[t + 1][:], in_=banks[("b", t + 1)][:])
+            if t + 2 < PACK:
+                nc.scalar.copy(out=a_rows[t + 2][:], in_=banks[("a", t + 2)][:])
+            nc.vector.tensor_tensor(out=pg[t][:], in0=pw[t][:], in1=pv[t][:], op=ADD)
+        for t in range(PACK):
+            pick(t)
+
+        floor = keep.tile([P, N // P, O], F32, tag="pg%d" % (PACK - 1))
+        for b in range(N // P):
+            nc.scalar.activation(
+                out=floor[:, b, :], in_=tz_rows[b][:].indirect(pick_tz[:]), func=COPY,
+                scale=so_cols[:, b : b + 1],
+            )
+
+        halves = [slice(h * HALF, (h + 1) * HALF) for h in range(2)]
+        hid = [keep.tile([P, HALF * PACK], BF16, align_bytes=64, name="hid%d" % h) for h in range(2)]
+        for h in range(2):
+            nc.vector.tensor_tensor(
+                out=hid[h][:].rearrange("p (c i t) -> p c t i", i=4, t=PACK),
+                in0=scaled[:, :, halves[h]].rearrange("p t (c i) -> p c t i", i=4),
+                in1=plain[:, :, halves[h]].rearrange("p t (c i) -> p c t i", i=4),
+                op=MAX,
+            )
+        sums = []
+        for h in range(2):
+            hid_codes = keep.tile([P, HALF], U32, align_bytes=64, name="hid_codes%d" % h)
+            hid_plane = keep.tile([P, HALF], U8, align_bytes=64, name="hid_plane%d" % h)
+            nc.vector.quantize_mx(out=hid_codes[:].bitcast(E5M2X4), scales=hid_plane[:], in_=hid[h][:])
+            bank = psum.tile([P, N // P, HALF], F32, name="bank_a%d" % h)
+            for b in range(N // P):
+                nc.tensor.matmul_mx(
+                    out=bank[:, b, :],
+                    lhsT=wb_codes[:, 2 * b * P : 2 * (b + 1) * P].bitcast(E2M1X4),
+                    lhsT_scale=wb_plane[:, b * P : (b + 1) * P],
+                    rhs=hid_codes[:].bitcast(E5M2X4),
+                    rhs_scale=hid_plane[:],
+                    start=True,
+                    stop=True,
+                )
+            sums.append(bank)
+        out_rows = out.rearrange("(b p) o -> p b o", p=P)
+        for h in range(2):
+            y = keep.tile([P, N // P, HALF], F32, name="y%d" % h)
+            nc.vector.tensor_tensor(out=y[:], in0=sums[h][:], in1=floor[:, :, halves[h]], op=MAX)
+            nc.sync.dma_start(out=out_rows[:, :, halves[h]], in_=y[:])

@@ -48,68 +48,71 @@ def tile_list_sumboardweighed_tied_one_stepfloor_kernel(
         w_plane = keep.tile([P, R], U8, align_bytes=64, tag="w_plane")
         xt_plane = keep.tile([P, T], U8, align_bytes=64, tag="xt_plane")
         wb_plane = keep.tile([P, N], U8, align_bytes=64)
-        nc.vector.memset(xt_plane[:].bitcast(I32), 0)
+        nc.gpsimd.memset(xt_plane[:].bitcast(I32), 0)
         nc.vector.memset(w_plane[:].bitcast(I32), 0)
 
+        w_stage = keep.tile([4, 4, R // 4], I32, align_bytes=64, tag="w_stage")
+        nc.scalar.dma_start(out=w_stage[:], in_=w_scales[0].bitcast(I32).rearrange("(q r) c -> r q c", r=4))
         xt_codes = keep.tile([P, T], U16, align_bytes=64, tag="xt_codes")
         nc.scalar.dma_start(out=xt_codes[:].bitcast(I32), in_=xt_words[0].bitcast(I32))
-        load_scale_rows(nc.scalar, xt_plane, xt_scales)
-        list_a = load_list("list_a", offs)
-        w_stage = keep.tile([4, 4, R // 4], I32, align_bytes=64, tag="w_stage")
-        nc.sync.dma_start(out=w_stage[:], in_=w_scales[0].bitcast(I32).rearrange("(q r) c -> r q c", r=4))
-        list_b = load_list("list_b", offs2)
-        put_a = load_list("put_a", offs3)
-        put_b = load_list("put_b", offs4)
-        pick_scaled = load_list("pick_scaled", offs5)
         w_codes = keep.tile([P, R], U32, align_bytes=64, tag="w_codes")
-        nc.sync.dma_start(
+        nc.scalar.dma_start(
             out=w_codes[:].bitcast(I32),
             in_=w_words[0].rearrange("p c t -> p (c t)").bitcast(I32),
         )
+        list_a = load_list("list_a", offs)
+        load_scale_rows(nc.sync, xt_plane, xt_scales)
+        list_b = load_list("list_b", offs2)
+        put_a = load_list("put_a", offs3)
+        put_b = load_list("put_b", offs4)
+        sa_cols = keep.tile([P, PACK], F32)
+        nc.sync.dma_start(out=sa_cols[:], in_=sa.rearrange("(p t) o -> p (t o)", t=PACK))
+        pick_scaled = load_list("pick_scaled", offs5)
         pick_plain = load_list("pick_plain", offs6)
         pick_tz = load_list("pick_tz", offs7)
 
-        pw = [keep.tile([P, C], F32, name="pw%d" % s) for s in range(2)] * 2
-        pv = [keep.tile([P, C], F32, name="pv%d" % s) for s in range(2)] * 2
-        for s in range(2):
-            nc.vector.memset(pw[s][:], 0.0)
-            nc.vector.memset(pv[s][:], 0.0)
+        pw = [keep.tile([P, C], F32, name="pw%d" % s) for s in range(3)]
+        pv = [keep.tile([P, C], F32, name="pv%d" % s) for s in range(2)]
+        for page in (pw[0], pv[0]):
+            nc.vector.memset(page[:], 0.0)
+        for page in (pw[1], pv[1], pw[2]):
+            nc.gpsimd.memset(page[:], 0.0)
+        pw = pw + pw[:1]
+        pv = pv + pv
         nc.vector.memset(wb_plane[:].bitcast(I32), 0)
         for q in range(4):
             nc.vector.tensor_copy(out=w_plane[32 * q : 32 * q + 4, :].bitcast(I32), in_=w_stage[:, q, :])
 
-        w_dealt = keep.tile([P, PACK, P], U32, align_bytes=64, tag="w_dealt")
-        nc.scalar.copy(
-            out=w_dealt[:].rearrange("p t m -> p m t"),
-            in_=w_codes[:].rearrange("p (m t) -> p m t", t=PACK),
-        )
+        w_dealt = [keep.tile([P, P], U32, align_bytes=64, name="w_dealt%d" % t) for t in range(PACK)]
+        for t in range(PACK):
+            nc.scalar.copy(out=w_dealt[t][:], in_=w_codes[:, t:R:PACK])
         w_plane_dealt = keep.tile([P, PACK, P], U8, align_bytes=64)
         nc.vector.tensor_copy(
             out=w_plane_dealt[:],
             in_=w_plane[:].rearrange("p (m t) -> p t m", t=PACK),
         )
 
+        groups = {"a": ((0,), (1,), (2, 3)), "b": ((0,), (1, 2), (3,))}
         banks = {}
         for side, picks in (("a", list_a), ("b", list_b)):
             codes = keep.tile([P, J], U16, align_bytes=64, name="codes_" + side)
             plane = keep.tile([P, J], U8, align_bytes=64, name="plane_" + side)
             nc.vector.tensor_copy(out=codes[:], in_=xt_codes[:].indirect(picks[:]))
             nc.vector.tensor_copy(out=plane[:], in_=xt_plane[:].indirect(picks[:]))
-            for t in range(PACK):
-                bank = psum.tile([P, J], F32, name="bank_%s%d" % (side, t))
-                nc.tensor.matmul_mx(
-                    out=bank[:],
-                    lhsT=w_dealt[:, t, :].bitcast(E4M3X4),
-                    lhsT_scale=w_plane_dealt[:, t, :],
-                    rhs=codes[:].bitcast(E2M1X4),
-                    rhs_scale=plane[:],
-                    start=True,
-                    stop=True,
-                )
-                banks[(side, t)] = bank
+            for group in groups[side]:
+                bank = psum.tile([P, len(group), J], F32, name="bank_%s%d" % (side, group[0]))
+                for place, t in enumerate(group):
+                    nc.tensor.matmul_mx(
+                        out=bank[:, place, :],
+                        lhsT=w_dealt[t][:].bitcast(E4M3X4),
+                        lhsT_scale=w_plane_dealt[:, t, :],
+                        rhs=codes[:].bitcast(E2M1X4),
+                        rhs_scale=plane[:],
+                        start=True,
+                        stop=True,
+                    )
+                banks[(side, group[0])] = bank
 
-        sa_cols = keep.tile([P, PACK], F32, align_bytes=64, tag="w_plane")
-        nc.sync.dma_start(out=sa_cols[:], in_=sa.rearrange("(p t) o -> p (t o)", t=PACK))
         wb_codes = keep.tile([P, 2 * N], U8, align_bytes=64, tag="xt_plane")
         nc.sync.dma_start(out=wb_codes[:].bitcast(I32), in_=wb_words[0].bitcast(I32))
         load_scale_rows(nc.sync, wb_plane, wb_scales)
@@ -122,35 +125,48 @@ def tile_list_sumboardweighed_tied_one_stepfloor_kernel(
             nc.sync.dma_start(out=rows[:], in_=tz[b * P : (b + 1) * P, :])
             tz_rows.append(rows)
 
-        a_rows = [keep.tile([P, J], F32, name="a_rows%d" % t) for t in range(PACK)]
-        b_rows = [keep.tile([P, J], F32, name="b_rows%d" % t) for t in range(PACK)]
+        rows_of = {}
+
+        def leave_bank(copy, side, first):
+            bank = banks[(side, first)]
+            rows = keep.tile(list(bank.shape), F32, name="rows_%s%d" % (side, first))
+            copy(out=rows[:], in_=bank[:])
+            for place in range(bank.shape[1]):
+                rows_of[(side, first + place)] = rows[:, place, :]
+
         pg = [keep.tile([P, C], F32, name="pg%d" % t, tag="pg%d" % t) for t in range(PACK)]
         scaled = keep.tile([P, PACK, O], F32)
         plain = keep.tile([P, PACK, O], F32)
 
-        def pick(t):
+        def pick(t, first, last, on_vector):
+            cols = slice(first, last)
+            entries = slice(first // 16, last // 16)
             nc.scalar.activation(
-                out=scaled[:, t, :], in_=pg[t][:].indirect(pick_scaled[:]), func=COPY,
+                out=scaled[:, t, cols], in_=pg[t][:].indirect(pick_scaled[:, entries]), func=COPY,
                 scale=sa_cols[:, t : t + 1],
             )
-            if t in (0, PACK - 1):
-                nc.vector.tensor_copy(out=plain[:, t, :], in_=pg[t][:].indirect(pick_plain[:]))
+            window = pg[t][:].indirect(pick_plain[:, entries])
+            if on_vector:
+                nc.vector.tensor_copy(out=plain[:, t, cols], in_=window)
             else:
-                nc.scalar.activation(out=plain[:, t, :], in_=pg[t][:].indirect(pick_plain[:]), func=COPY)
+                nc.scalar.activation(out=plain[:, t, cols], in_=window, func=COPY)
 
-        nc.scalar.copy(out=a_rows[0][:], in_=banks[("a", 0)][:])
-        nc.vector.tensor_copy(out=a_rows[1][:], in_=banks[("a", 1)][:])
-        nc.vector.tensor_copy(out=b_rows[0][:], in_=banks[("b", 0)][:])
+        leave_bank(nc.scalar.copy, "a", 0)
+        leave_bank(nc.vector.tensor_copy, "a", 1)
+        leave_bank(nc.vector.tensor_copy, "b", 0)
         for t in range(PACK):
-            nc.scalar.activation(out=pw[t][:].indirect(put_a[:]), in_=a_rows[t][:], func=COPY)
-            nc.vector.tensor_copy(out=pv[t][:].indirect(put_b[:]), in_=b_rows[t][:])
-            if t + 1 < PACK:
-                nc.scalar.copy(out=b_rows[t + 1][:], in_=banks[("b", t + 1)][:])
-            if t + 2 < PACK:
-                nc.scalar.copy(out=a_rows[t + 2][:], in_=banks[("a", t + 2)][:])
-            nc.vector.tensor_tensor(out=pg[t][:], in0=pw[t][:], in1=pv[t][:], op=ADD)
-        for t in range(PACK):
-            pick(t)
+            nc.scalar.activation(out=pw[t][:].indirect(put_a[:]), in_=rows_of[("a", t)], func=COPY)
+            if t == 0:
+                leave_bank(nc.scalar.copy, "a", 2)
+            nc.vector.tensor_copy(out=pv[t][:].indirect(put_b[:]), in_=rows_of[("b", t)])
+            if t in (0, 2):
+                leave_bank(nc.vector.tensor_copy, "b", t + 1)
+            adder = nc.gpsimd if t + 1 < PACK else nc.vector
+            adder.tensor_tensor(out=pg[t][:], in0=pw[t][:], in1=pv[t][:], op=ADD)
+        for t in range(PACK - 1):
+            pick(t, 0, O, t < 2)
+        pick(PACK - 1, 0, HALF, True)
+        pick(PACK - 1, HALF, O, False)
 
         floor = keep.tile([P, N // P, O], F32, tag="pg%d" % (PACK - 1))
         for b in range(N // P):

@@ -55,13 +55,13 @@ def tile_list_sumboardweighed_tied_one_stepfloor_kernel(
         nc.scalar.dma_start(out=w_stage[:], in_=w_scales[0].bitcast(I32).rearrange("(q r) c -> r q c", r=4))
         xt_codes = keep.tile([P, T], U16, align_bytes=64, tag="xt_codes")
         nc.scalar.dma_start(out=xt_codes[:].bitcast(I32), in_=xt_words[0].bitcast(I32))
+        list_a = load_list("list_a", offs)
+        load_scale_rows(nc.sync, xt_plane, xt_scales)
         w_codes = keep.tile([P, R], U32, align_bytes=64, tag="w_codes")
-        nc.scalar.dma_start(
+        nc.sync.dma_start(
             out=w_codes[:].bitcast(I32),
             in_=w_words[0].rearrange("p c t -> p (c t)").bitcast(I32),
         )
-        list_a = load_list("list_a", offs)
-        load_scale_rows(nc.sync, xt_plane, xt_scales)
         list_b = load_list("list_b", offs2)
         put_a = load_list("put_a", offs3)
         put_b = load_list("put_b", offs4)
@@ -72,13 +72,13 @@ def tile_list_sumboardweighed_tied_one_stepfloor_kernel(
         pick_tz = load_list("pick_tz", offs7)
 
         pw = [keep.tile([P, C], F32, name="pw%d" % s) for s in range(3)]
-        pv = [keep.tile([P, C], F32, name="pv%d" % s) for s in range(2)]
-        for page in (pw[0], pv[0]):
+        pv = [keep.tile([P, C], F32, name="pv%d" % s) for s in range(3)]
+        for page in (pw[0], pv[0], pv[2]):
             nc.vector.memset(page[:], 0.0)
         for page in (pw[1], pv[1], pw[2]):
             nc.gpsimd.memset(page[:], 0.0)
         pw = pw + pw[:1]
-        pv = pv + pv
+        pv = pv + pv[:1]
         nc.vector.memset(wb_plane[:].bitcast(I32), 0)
         for q in range(4):
             nc.vector.tensor_copy(out=w_plane[32 * q : 32 * q + 4, :].bitcast(I32), in_=w_stage[:, q, :])
@@ -86,11 +86,9 @@ def tile_list_sumboardweighed_tied_one_stepfloor_kernel(
         w_dealt = [keep.tile([P, P], U32, align_bytes=64, name="w_dealt%d" % t) for t in range(PACK)]
         for t in range(PACK):
             nc.scalar.copy(out=w_dealt[t][:], in_=w_codes[:, t:R:PACK])
-        w_plane_dealt = keep.tile([P, PACK, P], U8, align_bytes=64)
-        nc.vector.tensor_copy(
-            out=w_plane_dealt[:],
-            in_=w_plane[:].rearrange("p (m t) -> p t m", t=PACK),
-        )
+        w_plane_dealt = [keep.tile([P, P], U8, align_bytes=64, name="w_plane_dealt%d" % t) for t in range(PACK)]
+        for t in range(PACK):
+            nc.gpsimd.tensor_copy(out=w_plane_dealt[t][:], in_=w_plane[:, t:R:PACK])
 
         groups = {"a": ((0,), (1,), (2, 3)), "b": ((0,), (1, 2), (3,))}
         banks = {}
@@ -105,7 +103,7 @@ def tile_list_sumboardweighed_tied_one_stepfloor_kernel(
                     nc.tensor.matmul_mx(
                         out=bank[:, place, :],
                         lhsT=w_dealt[t][:].bitcast(E4M3X4),
-                        lhsT_scale=w_plane_dealt[:, t, :],
+                        lhsT_scale=w_plane_dealt[t][:],
                         rhs=codes[:].bitcast(E2M1X4),
                         rhs_scale=plane[:],
                         start=True,
@@ -138,14 +136,17 @@ def tile_list_sumboardweighed_tied_one_stepfloor_kernel(
         scaled = keep.tile([P, PACK, O], F32)
         plain = keep.tile([P, PACK, O], F32)
 
-        def pick(t, first, last, on_vector):
-            cols = slice(first, last)
-            entries = slice(first // 16, last // 16)
+        def pick_with_scale(t, first, last):
             nc.scalar.activation(
-                out=scaled[:, t, cols], in_=pg[t][:].indirect(pick_scaled[:, entries]), func=COPY,
+                out=scaled[:, t, first:last],
+                in_=pg[t][:].indirect(pick_scaled[:, first // 16 : last // 16]),
+                func=COPY,
                 scale=sa_cols[:, t : t + 1],
             )
-            window = pg[t][:].indirect(pick_plain[:, entries])
+
+        def pick_as_is(t, first, last, on_vector):
+            cols = slice(first, last)
+            window = pg[t][:].indirect(pick_plain[:, first // 16 : last // 16])
             if on_vector:
                 nc.vector.tensor_copy(out=plain[:, t, cols], in_=window)
             else:
@@ -161,12 +162,17 @@ def tile_list_sumboardweighed_tied_one_stepfloor_kernel(
             nc.vector.tensor_copy(out=pv[t][:].indirect(put_b[:]), in_=rows_of[("b", t)])
             if t in (0, 2):
                 leave_bank(nc.vector.tensor_copy, "b", t + 1)
-            adder = nc.gpsimd if t + 1 < PACK else nc.vector
-            adder.tensor_tensor(out=pg[t][:], in0=pw[t][:], in1=pv[t][:], op=ADD)
-        for t in range(PACK - 1):
-            pick(t, 0, O, t < 2)
-        pick(PACK - 1, 0, HALF, True)
-        pick(PACK - 1, HALF, O, False)
+            nc.gpsimd.tensor_tensor(out=pg[t][:], in0=pw[t][:], in1=pv[t][:], op=ADD)
+        for t in range(2):
+            pick_with_scale(t, 0, O)
+            pick_as_is(t, 0, O, True)
+        pick_with_scale(2, 0, O)
+        pick_as_is(2, 0, HALF, True)
+        pick_as_is(2, HALF, O, False)
+        pick_with_scale(3, 0, HALF)
+        pick_as_is(3, 0, HALF, True)
+        pick_with_scale(3, HALF, O)
+        pick_as_is(3, HALF, O, False)
 
         floor = keep.tile([P, N // P, O], F32, tag="pg%d" % (PACK - 1))
         for b in range(N // P):

@@ -54,9 +54,9 @@ def tile_list_sumboardweighed_tied_one_stepfloor_kernel(
         w_stage = keep.tile([4, 4, R // 4], I32, align_bytes=64, tag="w_stage")
         nc.scalar.dma_start(out=w_stage[:], in_=w_scales[0].bitcast(I32).rearrange("(q r) c -> r q c", r=4))
         xt_codes = keep.tile([P, T], U16, align_bytes=64, tag="xt_codes")
-        nc.scalar.dma_start(out=xt_codes[:].bitcast(I32), in_=xt_words[0].bitcast(I32))
         list_a = load_list("list_a", offs)
         load_scale_rows(nc.sync, xt_plane, xt_scales)
+        nc.sync.dma_start(out=xt_codes[:].bitcast(I32), in_=xt_words[0].bitcast(I32))
         w_codes = keep.tile([P, R], U32, align_bytes=64, tag="w_codes")
         nc.sync.dma_start(
             out=w_codes[:].bitcast(I32),
@@ -158,30 +158,31 @@ def tile_list_sumboardweighed_tied_one_stepfloor_kernel(
         for t in range(PACK):
             nc.scalar.activation(out=pw[t][:].indirect(put_a[:]), in_=rows_of[("a", t)], func=COPY)
             if t == 0:
+                leave_bank(nc.scalar.copy, "b", 1)
                 leave_bank(nc.scalar.copy, "a", 2)
             nc.vector.tensor_copy(out=pv[t][:].indirect(put_b[:]), in_=rows_of[("b", t)])
-            if t in (0, 2):
-                leave_bank(nc.vector.tensor_copy, "b", t + 1)
+            if t == 0:
+                leave_bank(nc.vector.tensor_copy, "b", 3)
             nc.gpsimd.tensor_tensor(out=pg[t][:], in0=pw[t][:], in1=pv[t][:], op=ADD)
-        for t in range(2):
+        for t in range(PACK - 1):
             pick_with_scale(t, 0, O)
             pick_as_is(t, 0, O, True)
-        pick_with_scale(2, 0, O)
-        pick_as_is(2, 0, HALF, True)
-        pick_as_is(2, HALF, O, False)
         pick_with_scale(3, 0, HALF)
         pick_as_is(3, 0, HALF, True)
         pick_with_scale(3, HALF, O)
         pick_as_is(3, HALF, O, False)
 
         floor = keep.tile([P, N // P, O], F32, tag="pg%d" % (PACK - 1))
-        for b in range(N // P):
-            nc.scalar.activation(
-                out=floor[:, b, :], in_=tz_rows[b][:].indirect(pick_tz[:]), func=COPY,
-                scale=so_cols[:, b : b + 1],
-            )
-
         halves = [slice(h * HALF, (h + 1) * HALF) for h in range(2)]
+        for h in range(2):
+            for b in range(N // P):
+                nc.scalar.activation(
+                    out=floor[:, b, halves[h]],
+                    in_=tz_rows[b][:].indirect(pick_tz[:, h * HALF // 16 : (h + 1) * HALF // 16]),
+                    func=COPY,
+                    scale=so_cols[:, b : b + 1],
+                )
+
         hid = [keep.tile([P, HALF * PACK], BF16, align_bytes=64, name="hid%d" % h) for h in range(2)]
         for h in range(2):
             nc.vector.tensor_tensor(

from contextlib import ExitStack

import concourse.mybir as mybir

K, T, J, R, C, O, N, E = 512, 2048, 256, 512, 512, 256, 256, 1024
FLOPS = 2 * K * R * 2 * J + 2 * R * N * O

F32 = mybir.dt.float32
BF16 = mybir.dt.bfloat16
I32 = mybir.dt.int32
U32 = mybir.dt.uint32
U16 = mybir.dt.uint16
U8 = mybir.dt.uint8
E4M3X4 = mybir.dt.float8_e4m3fn_x4
E5M2X4 = mybir.dt.float8_e5m2_x4
E2M1X4 = mybir.dt.float4_e2m1fn_x4
COPY = mybir.ActivationFunctionType.Copy
ADD = mybir.AluOpType.add
MAX = mybir.AluOpType.max

P = 128
PACK = 4
HALF = O // 2


def load_scale_rows(queue, plane, scales):
    for q in range(4):
        queue.dma_start(
            out=plane[32 * q : 32 * q + 4, :].bitcast(I32),
            in_=scales[0, 4 * q : 4 * q + 4, :].bitcast(I32),
        )


def tile_list_sumboardweighed_tied_one_stepfloor_kernel(
    tc, xt_words, xt_scales, w_words, w_scales, sa, wb_words, wb_scales, tz, so,
    offs, offs2, offs3, offs4, offs5, offs6, offs7, out,
):
    nc = tc.nc
    with ExitStack() as ctx:
        keep = ctx.enter_context(tc.tile_pool(name="keep", bufs=1))
        psum = ctx.enter_context(tc.psum_pool(name="psum", bufs=1))

        def load_list(name, src):
            tile = keep.tile([P, J // 16], U16, name=name)
            nc.sync.dma_start(tile[:], src)
            return tile

        w_plane = keep.tile([P, R], U8, align_bytes=64, tag="w_plane")
        xt_plane = keep.tile([P, T], U8, align_bytes=64, tag="xt_plane")
        wb_plane = keep.tile([P, N], U8, align_bytes=64)
        nc.gpsimd.memset(xt_plane[:].bitcast(I32), 0)
        nc.vector.memset(w_plane[:].bitcast(I32), 0)

        w_stage = keep.tile([4, 4, R // 4], I32, align_bytes=64, tag="w_stage")
        nc.scalar.dma_start(out=w_stage[:], in_=w_scales[0].bitcast(I32).rearrange("(q r) c -> r q c", r=4))
        xt_codes = keep.tile([P, T], U16, align_bytes=64, tag="xt_codes")
        list_a = load_list("list_a", offs)
        load_scale_rows(nc.sync, xt_plane, xt_scales)
        nc.sync.dma_start(out=xt_codes[:].bitcast(I32), in_=xt_words[0].bitcast(I32))
        w_codes = keep.tile([P, R], U32, align_bytes=64, tag="w_codes")
        nc.sync.dma_start(
            out=w_codes[:].bitcast(I32),
            in_=w_words[0].rearrange("p c t -> p (c t)").bitcast(I32),
        )
        list_b = load_list("list_b", offs2)
        put_a = load_list("put_a", offs3)
        put_b = load_list("put_b", offs4)
        sa_cols = keep.tile([P, PACK], F32)
        nc.sync.dma_start(out=sa_cols[:], in_=sa.rearrange("(p t) o -> p (t o)", t=PACK))
        pick_scaled = load_list("pick_scaled", offs5)
        pick_plain = load_list("pick_plain", offs6)
        pick_tz = load_list("pick_tz", offs7)

        pw = [keep.tile([P, C], F32, name="pw%d" % s) for s in range(3)]
        pv = [keep.tile([P, C], F32, name="pv%d" % s) for s in range(3)]
        for page in (pw[0], pv[0], pv[2]):
            nc.vector.memset(page[:], 0.0)
        for page in (pw[1], pv[1], pw[2]):
            nc.gpsimd.memset(page[:], 0.0)
        pw = pw + pw[:1]
        pv = pv + pv[:1]
        nc.vector.memset(wb_plane[:].bitcast(I32), 0)
        for q in range(4):
            nc.vector.tensor_copy(out=w_plane[32 * q : 32 * q + 4, :].bitcast(I32), in_=w_stage[:, q, :])

        w_dealt = [keep.tile([P, P], U32, align_bytes=64, name="w_dealt%d" % t) for t in range(PACK)]
        for t in range(PACK):
            nc.scalar.copy(out=w_dealt[t][:], in_=w_codes[:, t:R:PACK])
        w_plane_dealt = [keep.tile([P, P], U8, align_bytes=64, name="w_plane_dealt%d" % t) for t in range(PACK)]
        for t in range(PACK):
            nc.gpsimd.tensor_copy(out=w_plane_dealt[t][:], in_=w_plane[:, t:R:PACK])

        groups = {"a": ((0,), (1,), (2, 3)), "b": ((0,), (1, 2), (3,))}
        banks = {}
        for side, picks in (("a", list_a), ("b", list_b)):
            codes = keep.tile([P, J], U16, align_bytes=64, name="codes_" + side)
            plane = keep.tile([P, J], U8, align_bytes=64, name="plane_" + side)
            nc.vector.tensor_copy(out=codes[:], in_=xt_codes[:].indirect(picks[:]))
            nc.vector.tensor_copy(out=plane[:], in_=xt_plane[:].indirect(picks[:]))
            for group in groups[side]:
                bank = psum.tile([P, len(group), J], F32, name="bank_%s%d" % (side, group[0]))
                for place, t in enumerate(group):
                    nc.tensor.matmul_mx(
                        out=bank[:, place, :],
                        lhsT=w_dealt[t][:].bitcast(E4M3X4),
                        lhsT_scale=w_plane_dealt[t][:],
                        rhs=codes[:].bitcast(E2M1X4),
                        rhs_scale=plane[:],
                        start=True,
                        stop=True,
                    )
                banks[(side, group[0])] = bank

        wb_codes = keep.tile([P, 2 * N], U8, align_bytes=64, tag="xt_plane")
        nc.sync.dma_start(out=wb_codes[:].bitcast(I32), in_=wb_words[0].bitcast(I32))
        load_scale_rows(nc.sync, wb_plane, wb_scales)
        so_cols = keep.tile([P, N // P], F32, align_bytes=64, tag="w_stage")
        with nc.allow_non_contiguous_dma(reason="one step a partition"):
            nc.sync.dma_start(out=so_cols[:], in_=so.rearrange("(b p) o -> p (b o)", p=P))
        tz_rows = []
        for b in range(N // P):
            rows = keep.tile([P, E], F32, name="tz_rows%d" % b, align_bytes=64, tag=("w_codes", "xt_codes")[b])
            nc.sync.dma_start(out=rows[:], in_=tz[b * P : (b + 1) * P, :])
            tz_rows.append(rows)

        rows_of = {}

        def leave_bank(copy, side, first):
            bank = banks[(side, first)]
            rows = keep.tile(list(bank.shape), F32, name="rows_%s%d" % (side, first))
            copy(out=rows[:], in_=bank[:])
            for place in range(bank.shape[1]):
                rows_of[(side, first + place)] = rows[:, place, :]

        pg = [keep.tile([P, C], F32, name="pg%d" % t, tag="pg%d" % t) for t in range(PACK)]
        scaled = keep.tile([P, PACK, O], F32)
        plain = keep.tile([P, PACK, O], F32)

        def pick_with_scale(t, first, last):
            nc.scalar.activation(
                out=scaled[:, t, first:last],
                in_=pg[t][:].indirect(pick_scaled[:, first // 16 : last // 16]),
                func=COPY,
                scale=sa_cols[:, t : t + 1],
            )

        def pick_as_is(t, first, last, on_vector):
            cols = slice(first, last)
            window = pg[t][:].indirect(pick_plain[:, first // 16 : last // 16])
            if on_vector:
                nc.vector.tensor_copy(out=plain[:, t, cols], in_=window)
            else:
                nc.scalar.activation(out=plain[:, t, cols], in_=window, func=COPY)

        leave_bank(nc.scalar.copy, "a", 0)
        leave_bank(nc.vector.tensor_copy, "a", 1)
        leave_bank(nc.vector.tensor_copy, "b", 0)
        for t in range(PACK):
            nc.scalar.activation(out=pw[t][:].indirect(put_a[:]), in_=rows_of[("a", t)], func=COPY)
            if t == 0:
                leave_bank(nc.scalar.copy, "b", 1)
                leave_bank(nc.scalar.copy, "a", 2)
            nc.vector.tensor_copy(out=pv[t][:].indirect(put_b[:]), in_=rows_of[("b", t)])
            if t == 0:
                leave_bank(nc.vector.tensor_copy, "b", 3)
            nc.gpsimd.tensor_tensor(out=pg[t][:], in0=pw[t][:], in1=pv[t][:], op=ADD)
        for t in range(PACK - 1):
            pick_with_scale(t, 0, O)
            pick_as_is(t, 0, O, True)
        pick_with_scale(3, 0, HALF)
        pick_as_is(3, 0, HALF, True)
        pick_with_scale(3, HALF, O)
        pick_as_is(3, HALF, O, False)

        floor = keep.tile([P, N // P, O], F32, tag="pg%d" % (PACK - 1))
        halves = [slice(h * HALF, (h + 1) * HALF) for h in range(2)]
        for h in range(2):
            for b in range(N // P):
                nc.scalar.activation(
                    out=floor[:, b, halves[h]],
                    in_=tz_rows[b][:].indirect(pick_tz[:, h * HALF // 16 : (h + 1) * HALF // 16]),
                    func=COPY,
                    scale=so_cols[:, b : b + 1],
                )

        hid = [keep.tile([P, HALF * PACK], BF16, align_bytes=64, name="hid%d" % h) for h in range(2)]
        for h in range(2):
            nc.vector.tensor_tensor(
                out=hid[h][:].rearrange("p (c i t) -> p c t i", i=4, t=PACK),
                in0=scaled[:, :, halves[h]].rearrange("p t (c i) -> p c t i", i=4),
                in1=plain[:, :, halves[h]].rearrange("p t (c i) -> p c t i", i=4),
                op=MAX,
            )
        sums = []
        for h in range(2):
            hid_codes = keep.tile([P, HALF], U32, align_bytes=64, name="hid_codes%d" % h)
            hid_plane = keep.tile([P, HALF], U8, align_bytes=64, name="hid_plane%d" % h)
            nc.vector.quantize_mx(out=hid_codes[:].bitcast(E5M2X4), scales=hid_plane[:], in_=hid[h][:])
            bank = psum.tile([P, N // P, HALF], F32, name="bank_a%d" % h)
            for b in range(N // P):
                nc.tensor.matmul_mx(
                    out=bank[:, b, :],
                    lhsT=wb_codes[:, 2 * b * P : 2 * (b + 1) * P].bitcast(E2M1X4),
                    lhsT_scale=wb_plane[:, b * P : (b + 1) * P],
                    rhs=hid_codes[:].bitcast(E5M2X4),
                    rhs_scale=hid_plane[:],
                    start=True,
                    stop=True,
                )
            sums.append(bank)
        out_rows = out.rearrange("(b p) o -> p b o", p=P)
        for h in range(2):
            y = keep.tile([P, N // P, HALF], F32, name="y%d" % h)
            nc.vector.tensor_tensor(out=y[:], in0=sums[h][:], in1=floor[:, :, halves[h]], op=MAX)
            nc.sync.dma_start(out=out_rows[:, :, halves[h]], in_=y[:])
